import numpy as np
import ml_dtypes


def mxq(x, axis, fmt="e4m3"):
    dtype, down = {"e4m3": (ml_dtypes.float8_e4m3fn, 7), "e5m2": (ml_dtypes.float8_e5m2, 14)}[fmt]
    v = np.moveaxis(np.asarray(x, np.float32).astype(ml_dtypes.bfloat16).astype(np.float64), axis, -1)
    blocks = v.reshape(v.shape[:-1] + (-1, 32))
    amax = np.abs(blocks).max(-1, keepdims=True)
    byte = np.maximum(np.where(amax > 0, np.frexp(amax)[1] - 1 + 127, 0) - down, 1)
    scale = np.exp2(byte - 127.0)
    codes = (blocks / scale).astype(np.float32).astype(dtype).astype(np.float64)
    return np.moveaxis((codes * scale).reshape(v.shape), -1, axis)


WIDE = False


def mx_kscale(k):
    if not WIDE:
        return np.ones(k)
    levels = np.array([30, -30])
    if k % 512:
        return np.exp2(np.random.permutation(np.resize(levels, k // 32))).repeat(32)
    a = np.empty((k // 512, 16))
    for p in range(k // 512):
        a[p, :8] = np.random.permutation(np.resize(levels, 8))
        for g in range(8):
            far = levels[np.abs(levels - a[p, g]) >= 10]
            a[p, g + 8] = far[np.random.randint(len(far))]
    return np.exp2(a.ravel()).repeat(32)


def f64(x):
    return np.asarray(x).astype(np.float64)


def striped(idx):
    return np.tile(np.asarray(idx).reshape(-1, 16).T, (8, 1)).astype(np.uint16)


def unstriped(offs):
    return offs[:16].T.reshape(-1).astype(np.int64)


def striped8(idx):
    return np.asarray(idx).reshape(8, -1, 16).transpose(0, 2, 1).reshape(128, -1).astype(np.uint16)


def unstriped8(offs):
    return offs.reshape(8, 16, -1).transpose(0, 2, 1).reshape(8, -1).astype(np.int64)


def pick8(x, idx, run):
    r = np.arange(len(x))
    return x[r[:, None], idx[r % (8 * run) // run]]


E2M1 = np.array([0.0, 0.5, 1.0, 1.5, 2.0, 3.0, 4.0, 6.0, -0.0, -0.5, -1.0, -1.5, -2.0, -3.0, -4.0, -6.0])


def pack_weight(w, fmt):
    k, n = w.shape
    w = f64(np.asarray(w, np.float32).astype(ml_dtypes.bfloat16)).reshape(k // 32, 32, n)
    amax = np.abs(w).max(1)
    if fmt in ("e4m3", "e5m2"):
        byte = np.frexp(amax)[1] - 1 + 127 - (7 if fmt == "e4m3" else 14)
    else:
        mant, ex = np.frexp(amax / 6.0)
        byte = np.where(mant > 0.5, ex, ex - 1) + 127
    byte = np.clip(np.where(amax > 0, byte, 1), 1, 254)
    scaled = (w * np.exp2(127.0 - byte)[:, None, :]).reshape(k, n).astype(np.float32)
    by_word = np.ascontiguousarray(scaled.reshape(k // 512, 128, 4, n).transpose(0, 1, 3, 2))
    if fmt in ("e4m3", "e5m2"):
        words = by_word.astype(ml_dtypes.float8_e4m3fn if fmt == "e4m3" else ml_dtypes.float8_e5m2).view(np.uint8)
    else:
        c = by_word.astype(ml_dtypes.float4_e2m1fn).view(np.uint8) & 0xF
        words = (c[..., 0::2] | (c[..., 1::2] << 4)).reshape(k // 512, 128, 2 * n)
    return np.ascontiguousarray(words), np.ascontiguousarray(byte.astype(np.uint8).reshape(k // 512, 16, n))


def unpack_weight(words, scales, fmt):
    g, _, n = scales.shape
    words = np.ascontiguousarray(words).reshape(g, 128, n, -1)
    if fmt in ("e4m3", "e5m2"):
        vals = words.view(ml_dtypes.float8_e4m3fn if fmt == "e4m3" else ml_dtypes.float8_e5m2).astype(np.float64)
    else:
        nib = np.empty((g, 128, n, 4), np.uint8)
        nib[..., 0::2] = words & 0xF
        nib[..., 1::2] = words >> 4
        vals = E2M1[nib]
    vals = vals * np.repeat(np.exp2(scales.astype(np.float64) - 127.0), 8, axis=1)[..., None]
    return vals.transpose(0, 1, 3, 2).reshape(g * 512, n)


def sigmoid(v):
    return 1.0 / (1.0 + np.exp(-v))


def sgn(shape):
    return np.random.uniform(0.5, 2.0, shape) * np.where(np.random.standard_normal(shape) < 0, -1.0, 1.0)


K, T, J, R, F, Z, N, O = 512, 1024, 256, 512, 512, 1024, 256, 128


def setup_inputs():
    n = np.random.standard_normal
    idx = np.random.permutation(T)[:J]
    idx2 = np.random.permutation(Z)[:J]
    idx3 = np.stack([np.random.permutation(J)[:O] for _ in range(8)])
    idx4 = np.stack([np.random.permutation(J)[:O] for _ in range(8)])
    idx5 = np.random.permutation(J)[:O]
    fk = mx_kscale(K)
    ff = mx_kscale(F)
    fr = mx_kscale(R)
    xtp = pack_weight(n((K, T)) / fk[:, None], "e2m1")
    xop = pack_weight(n((F, Z)) / ff[:, None], "e4m3")
    wp = pack_weight(n((K, R)) * 1 / np.sqrt(K) * fk[:, None] * fr, "e4m3")
    w0p = pack_weight(n((F, R)) * 1 / np.sqrt(F) * ff[:, None] * fr, "e2m1")
    w2p = pack_weight(n((F, R)) * 1 / np.sqrt(F) * ff[:, None] * fr, "e5m2")
    wbp = pack_weight(n((R, N)) * 1 / np.sqrt(R) / fr[:, None], "e2m1")
    wcp = pack_weight(n((R, N)) * 1 / np.sqrt(R) / fr[:, None], "e5m2")
    return {
        "xt_words": xtp[0],
        "xt_scales": xtp[1],
        "xo_words": xop[0],
        "xo_scales": xop[1],
        "w_words": wp[0],
        "w_scales": wp[1],
        "w0_words": w0p[0],
        "w0_scales": w0p[1],
        "w2_words": w2p[0],
        "w2_scales": w2p[1],
        "wb_words": wbp[0],
        "wb_scales": wbp[1],
        "wc_words": wcp[0],
        "wc_scales": wcp[1],
        "so": (np.random.uniform(0.5, 1.6, (N, 1))).astype(np.float32),
        "sp": (sgn((N, 1))).astype(np.float32),
        "bo": (np.random.uniform(-2.0, 2.0, (N, 1))).astype(np.float32),
        "offs": striped(idx),
        "offs2": striped(idx2),
        "offs3": striped8(idx3),
        "offs4": striped8(idx4),
        "offs5": striped(idx5),
    }


def reference(xt_words, xt_scales, xo_words, xo_scales, w_words, w_scales, w0_words, w0_scales, w2_words, w2_scales, wb_words, wb_scales, wc_words, wc_scales, so, sp, bo, offs, offs2, offs3, offs4, offs5):
    idx = unstriped(offs)
    idx2 = unstriped(offs2)
    idx3 = unstriped8(offs3)
    idx4 = unstriped8(offs4)
    idx5 = unstriped(offs5)
    xtu = unpack_weight(xt_words, xt_scales, "e2m1")
    xou = unpack_weight(xo_words, xo_scales, "e4m3")
    wu = unpack_weight(w_words, w_scales, "e4m3")
    w0u = unpack_weight(w0_words, w0_scales, "e2m1")
    w2u = unpack_weight(w2_words, w2_scales, "e5m2")
    wbu = unpack_weight(wb_words, wb_scales, "e2m1")
    wcu = unpack_weight(wc_words, wc_scales, "e5m2")
    xtidxg = xtu[:, idx]
    xoidx2g = xou[:, idx2]
    a = wu.T @ xtidxg + w0u.T @ xoidx2g
    b = w2u.T @ xoidx2g
    hid = np.abs(a - b)
    hidq = mxq(hid, 0, "e5m2")
    p = wbu.T @ hidq
    q = wcu.T @ hidq
    y = pick8(p, idx3, 16) * f64(so) * sigmoid(pick8(p, idx4, 16) * f64(sp) + f64(bo)) - q[:, idx5]
    return y

@@ -1,0 +1,210 @@
+from contextlib import ExitStack
+
+import concourse.mybir as mybir
+from concourse.masks import make_identity
+
+F32 = mybir.dt.float32
+BF16 = mybir.dt.bfloat16
+I32 = mybir.dt.int32
+U32 = mybir.dt.uint32
+U16 = mybir.dt.uint16
+U8 = mybir.dt.uint8
+E4M3 = mybir.dt.float8_e4m3fn_x4
+E5M2 = mybir.dt.float8_e5m2_x4
+E2M1 = mybir.dt.float4_e2m1fn_x4
+ACT = mybir.ActivationFunctionType
+ALU = mybir.AluOpType
+
+P = 128
+T = 1024
+J = 256
+R = 512
+N = 256
+O = 128
+HALVES = J // P
+N_TILES = N // P
+FLOPS = 2 * 512 * R * J * 3 + 2 * R * N * J * 2
+
+
+def tile_list_outcomegatedgroups_noted_kernel(
+    tc, xt_words, xt_scales, xo_words, xo_scales, w_words, w_scales, w0_words, w0_scales,
+    w2_words, w2_scales, wb_words, wb_scales, wc_words, wc_scales, so, sp, bo,
+    offs, offs2, offs3, offs4, offs5, out,
+):
+    nc = tc.nc
+    with ExitStack() as ctx:
+        sb = ctx.enter_context(tc.tile_pool(name="sb", bufs=1))
+        ps = ctx.enter_context(tc.psum_pool(name="ps", bufs=1))
+
+        def tile(name, shape, dtype):
+            return sb.tile(shape, dtype, name=name, align_bytes=64)
+
+        def words_of(src):
+            flat = src[0] if len(src.shape) == 3 else src[0].rearrange("p n t -> p (n t)")
+            return flat.bitcast(I32)
+
+        def load_words(name, src, cols, dtype):
+            t = tile(name, [P, cols], dtype)
+            nc.sync.dma_start(out=t[:].bitcast(I32), in_=words_of(src))
+            return t
+
+        def load_list(name, src):
+            t = tile(name, [P, src.shape[1]], U16)
+            nc.sync.dma_start(t[:], src)
+            return t
+
+        def zeroed(name, cols, lo=0, hi=P, tag=None, engine=nc.vector):
+            t = sb.tile([P, cols], U8, name=name, tag=tag or name, align_bytes=64)
+            engine.memset(t[lo:hi, :].bitcast(I32), 0)
+            return t
+
+        def load_rows(stage, src):
+            nc.sync.dma_start(out=stage, in_=src[0].bitcast(I32).rearrange("(q r) n -> r q n", r=4))
+
+        def spread_rows(plane, stage):
+            for q in range(4):
+                nc.vector.tensor_copy(out=plane[32 * q:32 * q + 4, :].bitcast(I32), in_=stage[:, q, :])
+
+        def load_scale_pairs(t, src, base, queue):
+            rows = src[0].bitcast(I32).rearrange("(h b r) n -> b r h n", h=2, b=2)
+            view = t[:].bitcast(I32).rearrange("p (h n) -> p h n", h=2)
+            for b in range(2):
+                queue.dma_start(out=view[base + 32 * b:base + 32 * b + 4], in_=rows[b])
+
+        def lift_scale_pairs(t, cols):
+            view = t[:].bitcast(I32).rearrange("p (h n) -> p h n", h=2)
+            nc.vector.tensor_copy(out=view[64:128, 0, :], in_=view[0:64, 1, :])
+            return t[:, 0:cols]
+
+        xt_stage = zeroed("xt_stage", 2 * T, 64, P)
+        w_st = zeroed("w_st", 2 * R, 0, 64, engine=nc.gpsimd)
+        load_scale_pairs(w_st, w_scales, 0, nc.gpsimd)
+        xo_plane = zeroed("xo_plane", T)
+        w2_plane = zeroed("w2_plane", R)
+        w0_plane = zeroed("w0_plane", R)
+        ident = tile("ident", [P, P], F32)
+        make_identity(nc, ident[:])
+
+        xo_stage = tile("xo_stage", [4, 4, T // 4], I32)
+        load_rows(xo_stage[:], xo_scales)
+        l2 = load_list("l2", offs2)
+        w2_stage = tile("w2_stage", [4, 4, R // 4], I32)
+        load_rows(w2_stage[:], w2_scales)
+        xo_w = load_words("xo_w", xo_words, T, U32)
+        w2_w = load_words("w2_w", w2_words, R, U32)
+        load_scale_pairs(xt_stage, xt_scales, 64, nc.sync)
+        l1 = load_list("l1", offs)
+        w0_stage = tile("w0_stage", [4, 4, R // 4], I32)
+        load_rows(w0_stage[:], w0_scales)
+        w0_w = load_words("w0_w", w0_words, 2 * R, U8)
+        xt_w = load_words("xt_w", xt_words, T, U16)
+        w_w = load_words("w_w", w_words, R, U32)
+        out_stage = tile("out_stage", [4, 4, 2 * N // 4], I32)
+        load_rows(out_stage[:, :, 0:N // 4], wb_scales)
+        load_rows(out_stage[:, :, N // 4:2 * N // 4], wc_scales)
+        wb_w = load_words("wb_w", wb_words, 2 * N, U8)
+        wc_w = load_words("wc_w", wc_words, N, U32)
+        l4 = load_list("l4", offs4)
+        l3 = load_list("l3", offs3)
+        l5 = load_list("l5", offs5)
+        cols = []
+        with nc.allow_non_contiguous_dma(reason="one value a partition"):
+            for name, src in (("sp_c", sp), ("bo_c", bo), ("so_c", so)):
+                t = tile(name, [P, N_TILES], F32)
+                nc.sync.dma_start(out=t[:], in_=src.rearrange("(c p) o -> p (c o)", p=P))
+                cols.append(t)
+        sp_c, bo_c, so_c = cols
+
+        def half(lst, h):
+            return lst[:, h * (P // 16):(h + 1) * (P // 16)]
+
+        def slots(h):
+            return slice(h * P, (h + 1) * P)
+
+        spread_rows(xo_plane, xo_stage)
+        spread_rows(w2_plane, w2_stage)
+        xo_gs = [tile("xo_gs%d" % h, [P, P], U8) for h in range(HALVES)]
+        xo_g = [tile("xo_g%d" % h, [P, P], U32) for h in range(HALVES)]
+        w2_s = w2_plane[:]
+        b_ps = [ps.tile([P, R], F32, name="b_ps%d" % h) for h in range(HALVES)]
+        a_ps = [ps.tile([P, R], F32, name="a_ps%d" % h) for h in range(HALVES)]
+        b_sb = [tile("b_sb%d" % h, [P, 4, P], F32) for h in range(HALVES)]
+        for h in range(HALVES):
+            nc.vector.tensor_copy(out=xo_gs[h][:], in_=xo_plane[:].indirect(half(l2, h)))
+            nc.vector.tensor_copy(out=xo_g[h][:], in_=xo_w[:].indirect(half(l2, h)))
+            nc.tensor.matmul_mx(b_ps[h][:], lhsT=xo_g[h][:].bitcast(E4M3), lhsT_scale=xo_gs[h][:],
+                                rhs=w2_w[:].bitcast(E5M2), rhs_scale=w2_s, start=True, stop=True)
+            nc.scalar.copy(out=b_sb[h][:], in_=b_ps[h][:].rearrange("p (m t) -> p t m", t=4))
+
+        spread_rows(w0_plane, w0_stage)
+        w0_s = w0_plane[:]
+        xt_plane = tile("xt_plane", [P, T], U8)
+        stage_view = xt_stage[:].bitcast(I32).rearrange("p (h n) -> p h n", h=2)
+        for h in range(2):
+            nc.vector.tensor_copy(out=xt_plane[64 * h:64 * h + 64, :].bitcast(I32), in_=stage_view[64:128, h, :])
+        xt_gs = tile("xt_gs", [P, J], U8)
+        nc.vector.tensor_copy(out=xt_gs[:], in_=xt_plane[:].indirect(l1[:]))
+        w_s = lift_scale_pairs(w_st, R)
+        xt_g = [tile("xt_g%d" % h, [P, P], U16) for h in range(HALVES)]
+        for h in range(HALVES):
+            nc.tensor.matmul_mx(a_ps[h][:], lhsT=xo_g[h][:].bitcast(E4M3), lhsT_scale=xo_gs[h][:],
+                                rhs=w0_w[:].bitcast(E2M1), rhs_scale=w0_s, start=True, stop=False)
+            nc.vector.tensor_copy(out=xt_g[h][:], in_=xt_w[:].indirect(half(l1, h)))
+            nc.tensor.matmul_mx(a_ps[h][:], lhsT=xt_g[h][:].bitcast(E2M1), lhsT_scale=xt_gs[:, slots(h)],
+                                rhs=w_w[:].bitcast(E4M3), rhs_scale=w_s, start=False, stop=True)
+        out_plane = zeroed("out_plane", 2 * N, tag="xt_w")
+        spread_rows(out_plane, out_stage)
+        wb_s = out_plane[:, 0:N]
+        wc_s = out_plane[:, N:2 * N]
+
+        turned = [ps.tile([P, 4, P], F32, name="turned%d" % h) for h in range(HALVES)]
+        for h in range(HALVES):
+            a_view = a_ps[h][:].rearrange("p (m t) -> p t m", t=4)
+            for u in range(2):
+                diff = tile("diff%d%d" % (h, u), [P, 2, P], F32)
+                nc.vector.tensor_tensor(out=diff[:], in0=a_view[:, 2 * u:2 * u + 2], in1=b_sb[h][:, 2 * u:2 * u + 2],
+                                        op=ALU.subtract)
+                for e in range(2):
+                    nc.tensor.transpose(turned[h][:, 2 * u + e, :], diff[:, e, :], ident[:])
+
+        p_sb = [tile("p_sb%d" % c, [P, J], F32) for c in range(N_TILES)]
+        q_sb = tile("q_sb", [P, N_TILES, J], F32)
+        first = ps.tile([P, 4, P], F32, name="first")
+        last = ps.tile([P, P], F32, name="last")
+        p_ps = [[first[:, 0, :], first[:, 1, :]], [last[:], b_ps[0][:, 0:P]]]
+        q_ps = [first[:, 2:4, :], b_ps[1][:, 0:2 * P].rearrange("p (c j) -> p c j", c=2)]
+        for h in range(HALVES):
+            hid = tile("hid%d" % h, [P, P, 4], BF16)
+            nc.scalar.activation(out=hid[:], in_=turned[h][:].rearrange("p t j -> p j t"), func=ACT.Abs)
+            hq = tile("hq%d" % h, [P, P], U32)
+            hs = tile("hs%d" % h, [P, P], U8)
+            nc.vector.quantize_mx(out=hq[:].bitcast(E5M2), scales=hs[:], in_=hid[:].rearrange("p j t -> p (j t)"))
+            for c in range(N_TILES):
+                nc.tensor.matmul_mx(p_ps[h][c], lhsT=wb_w[:, 2 * P * c:2 * P * (c + 1)].bitcast(E2M1),
+                                    lhsT_scale=wb_s[:, slots(c)], rhs=hq[:].bitcast(E5M2), rhs_scale=hs[:],
+                                    start=True, stop=True)
+            for c in range(N_TILES):
+                nc.tensor.matmul_mx(q_ps[h][:, c, :], lhsT=wc_w[:, slots(c)].bitcast(E5M2),
+                                    lhsT_scale=wc_s[:, slots(c)], rhs=hq[:].bitcast(E5M2), rhs_scale=hs[:],
+                                    start=True, stop=True)
+        for c in range(N_TILES):
+            nc.scalar.copy(out=p_sb[c][:, slots(0)], in_=p_ps[0][c])
+        nc.vector.tensor_copy(out=q_sb[:, :, slots(0)], in_=q_ps[0])
+        nc.scalar.copy(out=p_sb[0][:, slots(1)], in_=p_ps[1][0])
+        nc.vector.tensor_copy(out=p_sb[1][:, slots(1)], in_=p_ps[1][1])
+        nc.vector.tensor_copy(out=q_sb[:, :, slots(1)], in_=q_ps[1])
+
+        for c in range(N_TILES):
+            gate = tile("gate%d" % c, [P, O], F32)
+            nc.scalar.activation(out=gate[:], in_=p_sb[c][:].indirect(l4[:]), func=ACT.Sigmoid,
+                                 bias=bo_c[:, c:c + 1], scale=sp_c[:, c:c + 1])
+            weighted = tile("weighted%d" % c, [P, O], F32)
+            nc.scalar.activation(out=weighted[:], in_=p_sb[c][:].indirect(l3[:]), func=ACT.Copy,
+                                 scale=so_c[:, c:c + 1])
+            picked = tile("picked%d" % c, [P, O], F32)
+            nc.vector.tensor_copy(out=picked[:], in_=q_sb[:, c, :].indirect(l5[:]))
+            gated = tile("gated%d" % c, [P, O], F32)
+            nc.vector.tensor_tensor(out=gated[:], in0=weighted[:], in1=gate[:], op=ALU.mult)
+            result = tile("result%d" % c, [P, O], F32)
+            nc.vector.tensor_tensor(out=result[:], in0=gated[:], in1=picked[:], op=ALU.subtract)
+            nc.sync.dma_start(out=out[slots(c), :], in_=result[:])

@@ -53,9 +53,9 @@ def tile_list_outcomegatedgroups_noted_kernel(
             nc.sync.dma_start(t[:], src)
             return t
 
-        def zeroed(name, cols, lo=0, hi=P, tag=None, engine=nc.vector):
+        def zeroed(name, cols, lo=0, hi=P, tag=None):
             t = sb.tile([P, cols], U8, name=name, tag=tag or name, align_bytes=64)
-            engine.memset(t[lo:hi, :].bitcast(I32), 0)
+            nc.vector.memset(t[lo:hi, :].bitcast(I32), 0)
             return t
 
         def load_rows(stage, src):
@@ -65,43 +65,46 @@ def tile_list_outcomegatedgroups_noted_kernel(
             for q in range(4):
                 nc.vector.tensor_copy(out=plane[32 * q:32 * q + 4, :].bitcast(I32), in_=stage[:, q, :])
 
-        def load_scale_pairs(t, src, base, queue):
+        def load_scale_pairs(t, src, base):
             rows = src[0].bitcast(I32).rearrange("(h b r) n -> b r h n", h=2, b=2)
             view = t[:].bitcast(I32).rearrange("p (h n) -> p h n", h=2)
             for b in range(2):
-                queue.dma_start(out=view[base + 32 * b:base + 32 * b + 4], in_=rows[b])
+                nc.sync.dma_start(out=view[base + 32 * b:base + 32 * b + 4], in_=rows[b])
 
-        def lift_scale_pairs(t, cols):
-            view = t[:].bitcast(I32).rearrange("p (h n) -> p h n", h=2)
-            nc.vector.tensor_copy(out=view[64:128, 0, :], in_=view[0:64, 1, :])
-            return t[:, 0:cols]
+        def plane_with_rows(name, cols):
+            t = tile(name, [P, 4 * cols], U8)
+            nc.vector.memset(t[:, 0:cols].bitcast(I32), 0)
+            return t[:, 0:cols], t[:].bitcast(I32).rearrange("p (q n) -> p q n", q=4)
 
+        def spread_in_place(rows):
+            for q in range(1, 4):
+                nc.vector.tensor_copy(out=rows[32 * q:32 * q + 4, 0, :], in_=rows[0:4, q, :])
+
+        w2_s, w2_rows = plane_with_rows("w2_plane", R)
         xt_stage = zeroed("xt_stage", 2 * T, 64, P)
-        w_st = zeroed("w_st", 2 * R, 0, 64, engine=nc.gpsimd)
-        load_scale_pairs(w_st, w_scales, 0, nc.gpsimd)
+        w_s, w_rows = plane_with_rows("w_plane", R)
         xo_plane = zeroed("xo_plane", T)
-        w2_plane = zeroed("w2_plane", R)
         w0_plane = zeroed("w0_plane", R)
+        out_plane, out_rows = plane_with_rows("out_plane", 2 * N)
         ident = tile("ident", [P, P], F32)
         make_identity(nc, ident[:])
 
         xo_stage = tile("xo_stage", [4, 4, T // 4], I32)
         load_rows(xo_stage[:], xo_scales)
         l2 = load_list("l2", offs2)
-        w2_stage = tile("w2_stage", [4, 4, R // 4], I32)
-        load_rows(w2_stage[:], w2_scales)
-        xo_w = load_words("xo_w", xo_words, T, U32)
-        w2_w = load_words("w2_w", w2_words, R, U32)
-        load_scale_pairs(xt_stage, xt_scales, 64, nc.sync)
-        l1 = load_list("l1", offs)
         w0_stage = tile("w0_stage", [4, 4, R // 4], I32)
         load_rows(w0_stage[:], w0_scales)
+        xo_w = load_words("xo_w", xo_words, T, U32)
         w0_w = load_words("w0_w", w0_words, 2 * R, U8)
+        load_rows(w2_rows[0:4], w2_scales)
+        load_scale_pairs(xt_stage, xt_scales, 64)
+        l1 = load_list("l1", offs)
+        w2_w = load_words("w2_w", w2_words, R, U32)
         xt_w = load_words("xt_w", xt_words, T, U16)
+        load_rows(w_rows[0:4], w_scales)
         w_w = load_words("w_w", w_words, R, U32)
-        out_stage = tile("out_stage", [4, 4, 2 * N // 4], I32)
-        load_rows(out_stage[:, :, 0:N // 4], wb_scales)
-        load_rows(out_stage[:, :, N // 4:2 * N // 4], wc_scales)
+        load_rows(out_rows[0:4, :, 0:N // 4], wb_scales)
+        load_rows(out_rows[0:4, :, N // 4:2 * N // 4], wc_scales)
         wb_w = load_words("wb_w", wb_words, 2 * N, U8)
         wc_w = load_words("wc_w", wc_words, N, U32)
         l4 = load_list("l4", offs4)
@@ -122,38 +125,43 @@ def tile_list_outcomegatedgroups_noted_kernel(
             return slice(h * P, (h + 1) * P)
 
         spread_rows(xo_plane, xo_stage)
-        spread_rows(w2_plane, w2_stage)
+        spread_rows(w0_plane, w0_stage)
+        w0_s = w0_plane[:]
         xo_gs = [tile("xo_gs%d" % h, [P, P], U8) for h in range(HALVES)]
         xo_g = [tile("xo_g%d" % h, [P, P], U32) for h in range(HALVES)]
-        w2_s = w2_plane[:]
         b_ps = [ps.tile([P, R], F32, name="b_ps%d" % h) for h in range(HALVES)]
         a_ps = [ps.tile([P, R], F32, name="a_ps%d" % h) for h in range(HALVES)]
         b_sb = [tile("b_sb%d" % h, [P, 4, P], F32) for h in range(HALVES)]
+
+        def notes_first(h):
+            nc.tensor.matmul_mx(a_ps[h][:], lhsT=xo_g[h][:].bitcast(E4M3), lhsT_scale=xo_gs[h][:],
+                                rhs=w0_w[:].bitcast(E2M1), rhs_scale=w0_s, start=True, stop=False)
+
         for h in range(HALVES):
             nc.vector.tensor_copy(out=xo_gs[h][:], in_=xo_plane[:].indirect(half(l2, h)))
             nc.vector.tensor_copy(out=xo_g[h][:], in_=xo_w[:].indirect(half(l2, h)))
+            if h == 0:
+                notes_first(h)
+                spread_in_place(w2_rows)
             nc.tensor.matmul_mx(b_ps[h][:], lhsT=xo_g[h][:].bitcast(E4M3), lhsT_scale=xo_gs[h][:],
                                 rhs=w2_w[:].bitcast(E5M2), rhs_scale=w2_s, start=True, stop=True)
             nc.scalar.copy(out=b_sb[h][:], in_=b_ps[h][:].rearrange("p (m t) -> p t m", t=4))
 
-        spread_rows(w0_plane, w0_stage)
-        w0_s = w0_plane[:]
+        notes_first(1)
+
         xt_plane = tile("xt_plane", [P, T], U8)
         stage_view = xt_stage[:].bitcast(I32).rearrange("p (h n) -> p h n", h=2)
         for h in range(2):
             nc.vector.tensor_copy(out=xt_plane[64 * h:64 * h + 64, :].bitcast(I32), in_=stage_view[64:128, h, :])
         xt_gs = tile("xt_gs", [P, J], U8)
         nc.vector.tensor_copy(out=xt_gs[:], in_=xt_plane[:].indirect(l1[:]))
-        w_s = lift_scale_pairs(w_st, R)
+        spread_in_place(w_rows)
         xt_g = [tile("xt_g%d" % h, [P, P], U16) for h in range(HALVES)]
         for h in range(HALVES):
-            nc.tensor.matmul_mx(a_ps[h][:], lhsT=xo_g[h][:].bitcast(E4M3), lhsT_scale=xo_gs[h][:],
-                                rhs=w0_w[:].bitcast(E2M1), rhs_scale=w0_s, start=True, stop=False)
             nc.vector.tensor_copy(out=xt_g[h][:], in_=xt_w[:].indirect(half(l1, h)))
             nc.tensor.matmul_mx(a_ps[h][:], lhsT=xt_g[h][:].bitcast(E2M1), lhsT_scale=xt_gs[:, slots(h)],
                                 rhs=w_w[:].bitcast(E4M3), rhs_scale=w_s, start=False, stop=True)
-        out_plane = zeroed("out_plane", 2 * N, tag="xt_w")
-        spread_rows(out_plane, out_stage)
+        spread_in_place(out_rows)
         wb_s = out_plane[:, 0:N]
         wc_s = out_plane[:, N:2 * N]
 

@@ -86,6 +86,10 @@ def tile_list_outcomegatedgroups_noted_kernel(
         xo_plane = zeroed("xo_plane", T)
         w0_plane = zeroed("w0_plane", R)
         out_plane, out_rows = plane_with_rows("out_plane", 2 * N)
+        warm_in = tile("warm_in", [P, 1], F32)
+        nc.gpsimd.memset(warm_in[:], 0.0)
+        warm_out = tile("warm_out", [P, 1], F32)
+        nc.scalar.activation(out=warm_out[:], in_=warm_in[:], func=ACT.Sigmoid)
         ident = tile("ident", [P, P], F32)
         make_identity(nc, ident[:])
 

@@ -16,14 +16,21 @@ ACT = mybir.ActivationFunctionType
 ALU = mybir.AluOpType
 
 P = 128
+K = 512
 T = 1024
 J = 256
 R = 512
 N = 256
 O = 128
+PACK = 4
+QUADS = 4
+QUAD = P // QUADS
+LIVE = 4
+WORD = 4
+GROUP = 16
 HALVES = J // P
 N_TILES = N // P
-FLOPS = 2 * 512 * R * J * 3 + 2 * R * N * J * 2
+FLOPS = 3 * 2 * K * R * J + 2 * 2 * R * N * J
 
 
 def tile_list_outcomegatedgroups_noted_kernel(
@@ -33,190 +40,177 @@ def tile_list_outcomegatedgroups_noted_kernel(
 ):
     nc = tc.nc
     with ExitStack() as ctx:
-        sb = ctx.enter_context(tc.tile_pool(name="sb", bufs=1))
-        ps = ctx.enter_context(tc.psum_pool(name="ps", bufs=1))
+        sbuf = ctx.enter_context(tc.tile_pool(name="sbuf", bufs=1))
+        psum = ctx.enter_context(tc.psum_pool(name="psum", bufs=1))
 
         def tile(name, shape, dtype):
-            return sb.tile(shape, dtype, name=name, align_bytes=64)
+            return sbuf.tile(shape, dtype, name=name, align_bytes=64)
 
-        def words_of(src):
-            flat = src[0] if len(src.shape) == 3 else src[0].rearrange("p n t -> p (n t)")
-            return flat.bitcast(I32)
+        def block(i):
+            return slice(i * P, (i + 1) * P)
 
         def load_words(name, src, cols, dtype):
-            t = tile(name, [P, cols], dtype)
-            nc.sync.dma_start(out=t[:].bitcast(I32), in_=words_of(src))
-            return t
+            words = tile(name, [P, cols], dtype)
+            flat = src[0] if len(src.shape) == 3 else src[0].rearrange("m c t -> m (c t)")
+            nc.sync.dma_start(out=words[:].bitcast(I32), in_=flat.bitcast(I32))
+            return words
 
         def load_list(name, src):
-            t = tile(name, [P, src.shape[1]], U16)
-            nc.sync.dma_start(t[:], src)
-            return t
+            entries = tile(name, [P, src.shape[1]], U16)
+            nc.sync.dma_start(entries[:], src)
+            return entries
 
-        def zeroed(name, cols, lo=0, hi=P, tag=None):
-            t = sb.tile([P, cols], U8, name=name, tag=tag or name, align_bytes=64)
-            nc.vector.memset(t[lo:hi, :].bitcast(I32), 0)
-            return t
+        def list_half(entries, h):
+            return entries[:, h * (P // GROUP):(h + 1) * (P // GROUP)]
 
-        def load_rows(stage, src):
-            nc.sync.dma_start(out=stage, in_=src[0].bitcast(I32).rearrange("(q r) n -> r q n", r=4))
+        def scale_rows(src):
+            return src[0].bitcast(I32).rearrange("(q i) c -> i q c", i=LIVE)
+
+        def zeroed_plane(name, cols):
+            plane = tile(name, [P, cols], U8)
+            nc.vector.memset(plane[:].bitcast(I32), 0)
+            return plane
 
         def spread_rows(plane, stage):
-            for q in range(4):
-                nc.vector.tensor_copy(out=plane[32 * q:32 * q + 4, :].bitcast(I32), in_=stage[:, q, :])
+            for q in range(QUADS):
+                nc.vector.tensor_copy(out=plane[QUAD * q:QUAD * q + LIVE, :].bitcast(I32), in_=stage[:, q, :])
 
-        def load_scale_pairs(t, src, base):
-            rows = src[0].bitcast(I32).rearrange("(h b r) n -> b r h n", h=2, b=2)
-            view = t[:].bitcast(I32).rearrange("p (h n) -> p h n", h=2)
-            for b in range(2):
-                nc.sync.dma_start(out=view[base + 32 * b:base + 32 * b + 4], in_=rows[b])
+        def plane_with_stage(name, cols):
+            both = tile(name, [P, QUADS * cols], U8)
+            nc.vector.memset(both[:, 0:cols].bitcast(I32), 0)
+            return both[:, 0:cols], both[:].bitcast(I32).rearrange("p (q c) -> p q c", q=QUADS)
 
-        def plane_with_rows(name, cols):
-            t = tile(name, [P, 4 * cols], U8)
-            nc.vector.memset(t[:, 0:cols].bitcast(I32), 0)
-            return t[:, 0:cols], t[:].bitcast(I32).rearrange("p (q n) -> p q n", q=4)
+        def spread_in_place(runs):
+            for q in range(1, QUADS):
+                nc.vector.tensor_copy(out=runs[QUAD * q:QUAD * q + LIVE, 0, :], in_=runs[0:LIVE, q, :])
 
-        def spread_in_place(rows):
-            for q in range(1, 4):
-                nc.vector.tensor_copy(out=rows[32 * q:32 * q + 4, 0, :], in_=rows[0:4, q, :])
+        xt_plane = zeroed_plane("xt_plane", T)
+        w_plane, w_runs = plane_with_stage("w_plane", R)
+        xo_plane = zeroed_plane("xo_plane", T)
+        w0_w2_plane = zeroed_plane("w0_w2_plane", 2 * R)
+        wb_wc_plane, wb_wc_runs = plane_with_stage("wb_wc_plane", 2 * N)
 
-        w2_s, w2_rows = plane_with_rows("w2_plane", R)
-        xt_stage = zeroed("xt_stage", 2 * T, 64, P)
-        w_s, w_rows = plane_with_rows("w_plane", R)
-        xo_plane = zeroed("xo_plane", T)
-        w0_plane = zeroed("w0_plane", R)
-        out_plane, out_rows = plane_with_rows("out_plane", 2 * N)
         warm_in = tile("warm_in", [P, 1], F32)
         nc.gpsimd.memset(warm_in[:], 0.0)
         warm_out = tile("warm_out", [P, 1], F32)
         nc.scalar.activation(out=warm_out[:], in_=warm_in[:], func=ACT.Sigmoid)
-        ident = tile("ident", [P, P], F32)
-        make_identity(nc, ident[:])
 
-        xo_stage = tile("xo_stage", [4, 4, T // 4], I32)
-        load_rows(xo_stage[:], xo_scales)
-        l2 = load_list("l2", offs2)
-        w0_stage = tile("w0_stage", [4, 4, R // 4], I32)
-        load_rows(w0_stage[:], w0_scales)
-        xo_w = load_words("xo_w", xo_words, T, U32)
-        w0_w = load_words("w0_w", w0_words, 2 * R, U8)
-        load_rows(w2_rows[0:4], w2_scales)
-        load_scale_pairs(xt_stage, xt_scales, 64)
-        l1 = load_list("l1", offs)
-        w2_w = load_words("w2_w", w2_words, R, U32)
-        xt_w = load_words("xt_w", xt_words, T, U16)
-        load_rows(w_rows[0:4], w_scales)
-        w_w = load_words("w_w", w_words, R, U32)
-        load_rows(out_rows[0:4, :, 0:N // 4], wb_scales)
-        load_rows(out_rows[0:4, :, N // 4:2 * N // 4], wc_scales)
-        wb_w = load_words("wb_w", wb_words, 2 * N, U8)
-        wc_w = load_words("wc_w", wc_words, N, U32)
-        l4 = load_list("l4", offs4)
-        l3 = load_list("l3", offs3)
-        l5 = load_list("l5", offs5)
-        cols = []
-        with nc.allow_non_contiguous_dma(reason="one value a partition"):
-            for name, src in (("sp_c", sp), ("bo_c", bo), ("so_c", so)):
-                t = tile(name, [P, N_TILES], F32)
-                nc.sync.dma_start(out=t[:], in_=src.rearrange("(c p) o -> p (c o)", p=P))
-                cols.append(t)
-        sp_c, bo_c, so_c = cols
+        identity = tile("identity", [P, P], F32)
+        make_identity(nc, identity[:])
 
-        def half(lst, h):
-            return lst[:, h * (P // 16):(h + 1) * (P // 16)]
-
-        def slots(h):
-            return slice(h * P, (h + 1) * P)
+        xo_stage = tile("xo_stage", [LIVE, QUADS, T // WORD], I32)
+        nc.sync.dma_start(out=xo_stage[:], in_=scale_rows(xo_scales))
+        note_list = load_list("note_list", offs2)
+        w0_w2_stage = tile("w0_w2_stage", [LIVE, QUADS, 2 * R // WORD], I32)
+        nc.sync.dma_start(out=w0_w2_stage[:, :, 0:R // WORD], in_=scale_rows(w0_scales))
+        nc.sync.dma_start(out=w0_w2_stage[:, :, R // WORD:2 * R // WORD], in_=scale_rows(w2_scales))
+        xo_sb = load_words("xo_sb", xo_words, T, U32)
+        w0_sb = load_words("w0_sb", w0_words, 2 * R, U8)
+        xt_rows = scale_rows(xt_scales)
+        for i in range(LIVE):
+            nc.sync.dma_start(out=xt_plane[i:P:QUAD, :].bitcast(I32), in_=xt_rows[i])
+        token_list = load_list("token_list", offs)
+        w2_sb = load_words("w2_sb", w2_words, R, U32)
+        nc.sync.dma_start(out=w_runs[0:LIVE], in_=scale_rows(w_scales))
+        xt_sb = load_words("xt_sb", xt_words, T, U16)
+        w_sb = load_words("w_sb", w_words, R, U32)
+        nc.sync.dma_start(out=wb_wc_runs[0:LIVE, :, 0:N // WORD], in_=scale_rows(wb_scales))
+        nc.sync.dma_start(out=wb_wc_runs[0:LIVE, :, N // WORD:2 * N // WORD], in_=scale_rows(wc_scales))
+        wb_sb = load_words("wb_sb", wb_words, 2 * N, U8)
+        wc_sb = load_words("wc_sb", wc_words, N, U32)
+        gate_lists = load_list("gate_lists", offs4)
+        weighted_lists = load_list("weighted_lists", offs3)
+        q_list = load_list("q_list", offs5)
+        per_feature = []
+        with nc.allow_non_contiguous_dma(reason="column c holds the value of output feature 128 c + p on partition p"):
+            for name, src in (("sp_sb", sp), ("bo_sb", bo), ("so_sb", so)):
+                values = tile(name, [P, N_TILES], F32)
+                nc.sync.dma_start(out=values[:], in_=src.rearrange("(c p) o -> p (c o)", p=P))
+                per_feature.append(values)
+        sp_sb, bo_sb, so_sb = per_feature
 
         spread_rows(xo_plane, xo_stage)
-        spread_rows(w0_plane, w0_stage)
-        w0_s = w0_plane[:]
-        xo_gs = [tile("xo_gs%d" % h, [P, P], U8) for h in range(HALVES)]
-        xo_g = [tile("xo_g%d" % h, [P, P], U32) for h in range(HALVES)]
-        b_ps = [ps.tile([P, R], F32, name="b_ps%d" % h) for h in range(HALVES)]
-        a_ps = [ps.tile([P, R], F32, name="a_ps%d" % h) for h in range(HALVES)]
-        b_sb = [tile("b_sb%d" % h, [P, 4, P], F32) for h in range(HALVES)]
-
-        def notes_first(h):
-            nc.tensor.matmul_mx(a_ps[h][:], lhsT=xo_g[h][:].bitcast(E4M3), lhsT_scale=xo_gs[h][:],
-                                rhs=w0_w[:].bitcast(E2M1), rhs_scale=w0_s, start=True, stop=False)
-
+        spread_rows(w0_w2_plane, w0_w2_stage)
+        w0_plane = w0_w2_plane[:, 0:R]
+        w2_plane = w0_w2_plane[:, R:2 * R]
+        note_scales = tile("note_scales", [P, J], U8)
+        nc.vector.tensor_copy(out=note_scales[:], in_=xo_plane[:].indirect(note_list[:]))
+        note_words = [tile("note_words%d" % h, [P, P], U32) for h in range(HALVES)]
+        b_ps = [psum.tile([P, R], F32, name="b_ps%d" % h) for h in range(HALVES)]
+        a_ps = [psum.tile([P, R], F32, name="a_ps%d" % h) for h in range(HALVES)]
+        b_sb = [tile("b_sb%d" % h, [P, PACK, P], F32) for h in range(HALVES)]
         for h in range(HALVES):
-            nc.vector.tensor_copy(out=xo_gs[h][:], in_=xo_plane[:].indirect(half(l2, h)))
-            nc.vector.tensor_copy(out=xo_g[h][:], in_=xo_w[:].indirect(half(l2, h)))
-            if h == 0:
-                notes_first(h)
-                spread_in_place(w2_rows)
-            nc.tensor.matmul_mx(b_ps[h][:], lhsT=xo_g[h][:].bitcast(E4M3), lhsT_scale=xo_gs[h][:],
-                                rhs=w2_w[:].bitcast(E5M2), rhs_scale=w2_s, start=True, stop=True)
-            nc.scalar.copy(out=b_sb[h][:], in_=b_ps[h][:].rearrange("p (m t) -> p t m", t=4))
-
-        notes_first(1)
-
-        xt_plane = tile("xt_plane", [P, T], U8)
-        stage_view = xt_stage[:].bitcast(I32).rearrange("p (h n) -> p h n", h=2)
-        for h in range(2):
-            nc.vector.tensor_copy(out=xt_plane[64 * h:64 * h + 64, :].bitcast(I32), in_=stage_view[64:128, h, :])
-        xt_gs = tile("xt_gs", [P, J], U8)
-        nc.vector.tensor_copy(out=xt_gs[:], in_=xt_plane[:].indirect(l1[:]))
-        spread_in_place(w_rows)
-        xt_g = [tile("xt_g%d" % h, [P, P], U16) for h in range(HALVES)]
+            nc.vector.tensor_copy(out=note_words[h][:], in_=xo_sb[:].indirect(list_half(note_list, h)))
+            nc.tensor.matmul_mx(a_ps[h][:], lhsT=note_words[h][:].bitcast(E4M3), lhsT_scale=note_scales[:, block(h)],
+                                rhs=w0_sb[:].bitcast(E2M1), rhs_scale=w0_plane, start=True, stop=False)
         for h in range(HALVES):
-            nc.vector.tensor_copy(out=xt_g[h][:], in_=xt_w[:].indirect(half(l1, h)))
-            nc.tensor.matmul_mx(a_ps[h][:], lhsT=xt_g[h][:].bitcast(E2M1), lhsT_scale=xt_gs[:, slots(h)],
-                                rhs=w_w[:].bitcast(E4M3), rhs_scale=w_s, start=False, stop=True)
-        spread_in_place(out_rows)
-        wb_s = out_plane[:, 0:N]
-        wc_s = out_plane[:, N:2 * N]
+            nc.tensor.matmul_mx(b_ps[h][:], lhsT=note_words[h][:].bitcast(E4M3), lhsT_scale=note_scales[:, block(h)],
+                                rhs=w2_sb[:].bitcast(E5M2), rhs_scale=w2_plane, start=True, stop=True)
+            nc.scalar.copy(out=b_sb[h][:], in_=b_ps[h][:].rearrange("j (m t) -> j t m", t=PACK))
 
-        turned = [ps.tile([P, 4, P], F32, name="turned%d" % h) for h in range(HALVES)]
+        token_scales = tile("token_scales", [P, J], U8)
+        nc.vector.tensor_copy(out=token_scales[:], in_=xt_plane[:].indirect(token_list[:]))
+        spread_in_place(w_runs)
+        token_words = [tile("token_words%d" % h, [P, P], U16) for h in range(HALVES)]
         for h in range(HALVES):
-            a_view = a_ps[h][:].rearrange("p (m t) -> p t m", t=4)
-            for u in range(2):
-                diff = tile("diff%d%d" % (h, u), [P, 2, P], F32)
-                nc.vector.tensor_tensor(out=diff[:], in0=a_view[:, 2 * u:2 * u + 2], in1=b_sb[h][:, 2 * u:2 * u + 2],
-                                        op=ALU.subtract)
+            nc.vector.tensor_copy(out=token_words[h][:], in_=xt_sb[:].indirect(list_half(token_list, h)))
+            nc.tensor.matmul_mx(a_ps[h][:], lhsT=token_words[h][:].bitcast(E2M1), lhsT_scale=token_scales[:, block(h)],
+                                rhs=w_sb[:].bitcast(E4M3), rhs_scale=w_plane, start=False, stop=True)
+        spread_in_place(wb_wc_runs)
+        wb_plane = wb_wc_plane[:, 0:N]
+        wc_plane = wb_wc_plane[:, N:2 * N]
+
+        turned = [psum.tile([P, PACK, P], F32, name="turned%d" % h) for h in range(HALVES)]
+        for h in range(HALVES):
+            a_by_t = a_ps[h][:].rearrange("j (m t) -> j t m", t=PACK)
+            for pair in range(PACK // 2):
+                ts = slice(2 * pair, 2 * pair + 2)
+                diff = tile("diff%d%d" % (h, pair), [P, 2, P], F32)
+                nc.vector.tensor_tensor(out=diff[:], in0=a_by_t[:, ts], in1=b_sb[h][:, ts], op=ALU.subtract)
                 for e in range(2):
-                    nc.tensor.transpose(turned[h][:, 2 * u + e, :], diff[:, e, :], ident[:])
+                    nc.tensor.transpose(turned[h][:, 2 * pair + e, :], diff[:, e, :], identity[:])
 
         p_sb = [tile("p_sb%d" % c, [P, J], F32) for c in range(N_TILES)]
         q_sb = tile("q_sb", [P, N_TILES, J], F32)
-        first = ps.tile([P, 4, P], F32, name="first")
-        last = ps.tile([P, P], F32, name="last")
-        p_ps = [[first[:, 0, :], first[:, 1, :]], [last[:], b_ps[0][:, 0:P]]]
-        q_ps = [first[:, 2:4, :], b_ps[1][:, 0:2 * P].rearrange("p (c j) -> p c j", c=2)]
+        first_half_ps = psum.tile([P, 2 * N_TILES, P], F32, name="first_half_ps")
+        last_half_ps = psum.tile([P, P], F32, name="last_half_ps")
+        p_ps = [[first_half_ps[:, 0, :], first_half_ps[:, 1, :]], [last_half_ps[:], b_ps[0][:, 0:P]]]
+        q_ps = [first_half_ps[:, N_TILES:2 * N_TILES, :],
+                b_ps[1][:, 0:N_TILES * P].rearrange("n (c j) -> n c j", c=N_TILES)]
         for h in range(HALVES):
-            hid = tile("hid%d" % h, [P, P, 4], BF16)
-            nc.scalar.activation(out=hid[:], in_=turned[h][:].rearrange("p t j -> p j t"), func=ACT.Abs)
-            hq = tile("hq%d" % h, [P, P], U32)
-            hs = tile("hs%d" % h, [P, P], U8)
-            nc.vector.quantize_mx(out=hq[:].bitcast(E5M2), scales=hs[:], in_=hid[:].rearrange("p j t -> p (j t)"))
+            hid = tile("hid%d" % h, [P, P, PACK], BF16)
+            nc.scalar.activation(out=hid[:], in_=turned[h][:].rearrange("m t j -> m j t"), func=ACT.Abs)
+            hid_words = tile("hid_words%d" % h, [P, P], U32)
+            hid_plane = tile("hid_plane%d" % h, [P, P], U8)
+            nc.vector.quantize_mx(out=hid_words[:].bitcast(E5M2), scales=hid_plane[:],
+                                  in_=hid[:].rearrange("m j t -> m (j t)"))
             for c in range(N_TILES):
-                nc.tensor.matmul_mx(p_ps[h][c], lhsT=wb_w[:, 2 * P * c:2 * P * (c + 1)].bitcast(E2M1),
-                                    lhsT_scale=wb_s[:, slots(c)], rhs=hq[:].bitcast(E5M2), rhs_scale=hs[:],
-                                    start=True, stop=True)
+                nc.tensor.matmul_mx(p_ps[h][c], lhsT=wb_sb[:, 2 * P * c:2 * P * (c + 1)].bitcast(E2M1),
+                                    lhsT_scale=wb_plane[:, block(c)], rhs=hid_words[:].bitcast(E5M2),
+                                    rhs_scale=hid_plane[:], start=True, stop=True)
             for c in range(N_TILES):
-                nc.tensor.matmul_mx(q_ps[h][:, c, :], lhsT=wc_w[:, slots(c)].bitcast(E5M2),
-                                    lhsT_scale=wc_s[:, slots(c)], rhs=hq[:].bitcast(E5M2), rhs_scale=hs[:],
-                                    start=True, stop=True)
+                nc.tensor.matmul_mx(q_ps[h][:, c, :], lhsT=wc_sb[:, block(c)].bitcast(E5M2),
+                                    lhsT_scale=wc_plane[:, block(c)], rhs=hid_words[:].bitcast(E5M2),
+                                    rhs_scale=hid_plane[:], start=True, stop=True)
+
         for c in range(N_TILES):
-            nc.scalar.copy(out=p_sb[c][:, slots(0)], in_=p_ps[0][c])
-        nc.vector.tensor_copy(out=q_sb[:, :, slots(0)], in_=q_ps[0])
-        nc.scalar.copy(out=p_sb[0][:, slots(1)], in_=p_ps[1][0])
-        nc.vector.tensor_copy(out=p_sb[1][:, slots(1)], in_=p_ps[1][1])
-        nc.vector.tensor_copy(out=q_sb[:, :, slots(1)], in_=q_ps[1])
+            nc.scalar.copy(out=p_sb[c][:, block(0)], in_=p_ps[0][c])
+        nc.vector.tensor_copy(out=q_sb[:, :, block(0)], in_=q_ps[0])
+        nc.scalar.copy(out=p_sb[0][:, block(1)], in_=p_ps[1][0])
+        nc.vector.tensor_copy(out=p_sb[1][:, block(1)], in_=p_ps[1][1])
+        nc.vector.tensor_copy(out=q_sb[:, :, block(1)], in_=q_ps[1])
 
         for c in range(N_TILES):
             gate = tile("gate%d" % c, [P, O], F32)
-            nc.scalar.activation(out=gate[:], in_=p_sb[c][:].indirect(l4[:]), func=ACT.Sigmoid,
-                                 bias=bo_c[:, c:c + 1], scale=sp_c[:, c:c + 1])
+            nc.scalar.activation(out=gate[:], in_=p_sb[c][:].indirect(gate_lists[:]), func=ACT.Sigmoid,
+                                 bias=bo_sb[:, c:c + 1], scale=sp_sb[:, c:c + 1])
             weighted = tile("weighted%d" % c, [P, O], F32)
-            nc.scalar.activation(out=weighted[:], in_=p_sb[c][:].indirect(l3[:]), func=ACT.Copy,
-                                 scale=so_c[:, c:c + 1])
+            nc.scalar.activation(out=weighted[:], in_=p_sb[c][:].indirect(weighted_lists[:]), func=ACT.Copy,
+                                 scale=so_sb[:, c:c + 1])
             picked = tile("picked%d" % c, [P, O], F32)
-            nc.vector.tensor_copy(out=picked[:], in_=q_sb[:, c, :].indirect(l5[:]))
+            nc.vector.tensor_copy(out=picked[:], in_=q_sb[:, c, :].indirect(q_list[:]))
             gated = tile("gated%d" % c, [P, O], F32)
             nc.vector.tensor_tensor(out=gated[:], in0=weighted[:], in1=gate[:], op=ALU.mult)
             result = tile("result%d" % c, [P, O], F32)
             nc.vector.tensor_tensor(out=result[:], in0=gated[:], in1=picked[:], op=ALU.subtract)
-            nc.sync.dma_start(out=out[slots(c), :], in_=result[:])
+            nc.sync.dma_start(out=out[block(c), :], in_=result[:])

@@ -71,6 +71,11 @@ def tile_list_outcomegatedgroups_noted_kernel(
             nc.vector.memset(plane[:].bitcast(I32), 0)
             return plane
 
+        def load_plane(plane, src):
+            rows = scale_rows(src)
+            for i in range(LIVE):
+                nc.sync.dma_start(out=plane[i:P:QUAD, :].bitcast(I32), in_=rows[i])
+
         def spread_rows(plane, stage):
             for q in range(QUADS):
                 nc.vector.tensor_copy(out=plane[QUAD * q:QUAD * q + LIVE, :].bitcast(I32), in_=stage[:, q, :])
@@ -85,7 +90,7 @@ def tile_list_outcomegatedgroups_noted_kernel(
                 nc.vector.tensor_copy(out=runs[QUAD * q:QUAD * q + LIVE, 0, :], in_=runs[0:LIVE, q, :])
 
         xt_plane = zeroed_plane("xt_plane", T)
-        w_plane, w_runs = plane_with_stage("w_plane", R)
+        w_plane = zeroed_plane("w_plane", R)
         xo_plane = zeroed_plane("xo_plane", T)
         w0_w2_plane = zeroed_plane("w0_w2_plane", 2 * R)
         wb_wc_plane, wb_wc_runs = plane_with_stage("wb_wc_plane", 2 * N)
@@ -106,14 +111,12 @@ def tile_list_outcomegatedgroups_noted_kernel(
         nc.sync.dma_start(out=w0_w2_stage[:, :, R // WORD:2 * R // WORD], in_=scale_rows(w2_scales))
         xo_sb = load_words("xo_sb", xo_words, T, U32)
         w0_sb = load_words("w0_sb", w0_words, 2 * R, U8)
-        xt_rows = scale_rows(xt_scales)
-        for i in range(LIVE):
-            nc.sync.dma_start(out=xt_plane[i:P:QUAD, :].bitcast(I32), in_=xt_rows[i])
+        load_plane(xt_plane, xt_scales)
         token_list = load_list("token_list", offs)
         w2_sb = load_words("w2_sb", w2_words, R, U32)
-        nc.sync.dma_start(out=w_runs[0:LIVE], in_=scale_rows(w_scales))
         xt_sb = load_words("xt_sb", xt_words, T, U16)
         w_sb = load_words("w_sb", w_words, R, U32)
+        load_plane(w_plane, w_scales)
         nc.sync.dma_start(out=wb_wc_runs[0:LIVE, :, 0:N // WORD], in_=scale_rows(wb_scales))
         nc.sync.dma_start(out=wb_wc_runs[0:LIVE, :, N // WORD:2 * N // WORD], in_=scale_rows(wc_scales))
         wb_sb = load_words("wb_sb", wb_words, 2 * N, U8)
@@ -150,12 +153,11 @@ def tile_list_outcomegatedgroups_noted_kernel(
 
         token_scales = tile("token_scales", [P, J], U8)
         nc.vector.tensor_copy(out=token_scales[:], in_=xt_plane[:].indirect(token_list[:]))
-        spread_in_place(w_runs)
         token_words = [tile("token_words%d" % h, [P, P], U16) for h in range(HALVES)]
         for h in range(HALVES):
             nc.vector.tensor_copy(out=token_words[h][:], in_=xt_sb[:].indirect(list_half(token_list, h)))
             nc.tensor.matmul_mx(a_ps[h][:], lhsT=token_words[h][:].bitcast(E2M1), lhsT_scale=token_scales[:, block(h)],
-                                rhs=w_sb[:].bitcast(E4M3), rhs_scale=w_plane, start=False, stop=True)
+                                rhs=w_sb[:].bitcast(E4M3), rhs_scale=w_plane[:], start=False, stop=True)
         spread_in_place(wb_wc_runs)
         wb_plane = wb_wc_plane[:, 0:N]
         wc_plane = wb_wc_plane[:, N:2 * N]

from contextlib import ExitStack

import concourse.mybir as mybir
from concourse.masks import make_identity

F32 = mybir.dt.float32
BF16 = mybir.dt.bfloat16
I32 = mybir.dt.int32
U32 = mybir.dt.uint32
U16 = mybir.dt.uint16
U8 = mybir.dt.uint8
E4M3 = mybir.dt.float8_e4m3fn_x4
E5M2 = mybir.dt.float8_e5m2_x4
E2M1 = mybir.dt.float4_e2m1fn_x4
ACT = mybir.ActivationFunctionType
ALU = mybir.AluOpType

P = 128
K = 512
T = 1024
J = 256
R = 512
N = 256
O = 128
PACK = 4
QUADS = 4
QUAD = P // QUADS
LIVE = 4
WORD = 4
GROUP = 16
HALVES = J // P
N_TILES = N // P
FLOPS = 3 * 2 * K * R * J + 2 * 2 * R * N * J


def tile_list_outcomegatedgroups_noted_kernel(
    tc, xt_words, xt_scales, xo_words, xo_scales, w_words, w_scales, w0_words, w0_scales,
    w2_words, w2_scales, wb_words, wb_scales, wc_words, wc_scales, so, sp, bo,
    offs, offs2, offs3, offs4, offs5, out,
):
    nc = tc.nc
    with ExitStack() as ctx:
        sbuf = ctx.enter_context(tc.tile_pool(name="sbuf", bufs=1))
        psum = ctx.enter_context(tc.psum_pool(name="psum", bufs=1))

        def tile(name, shape, dtype):
            return sbuf.tile(shape, dtype, name=name, align_bytes=64)

        def block(i):
            return slice(i * P, (i + 1) * P)

        def load_words(name, src, cols, dtype):
            words = tile(name, [P, cols], dtype)
            flat = src[0] if len(src.shape) == 3 else src[0].rearrange("m c t -> m (c t)")
            nc.sync.dma_start(out=words[:].bitcast(I32), in_=flat.bitcast(I32))
            return words

        def load_list(name, src):
            entries = tile(name, [P, src.shape[1]], U16)
            nc.sync.dma_start(entries[:], src)
            return entries

        def list_half(entries, h):
            return entries[:, h * (P // GROUP):(h + 1) * (P // GROUP)]

        def scale_rows(src):
            return src[0].bitcast(I32).rearrange("(q i) c -> i q c", i=LIVE)

        def zeroed_plane(name, cols):
            plane = tile(name, [P, cols], U8)
            nc.vector.memset(plane[:].bitcast(I32), 0)
            return plane

        def load_plane(plane, src):
            rows = scale_rows(src)
            for i in range(LIVE):
                nc.sync.dma_start(out=plane[i:P:QUAD, :].bitcast(I32), in_=rows[i])

        def spread_rows(plane, stage):
            for q in range(QUADS):
                nc.vector.tensor_copy(out=plane[QUAD * q:QUAD * q + LIVE, :].bitcast(I32), in_=stage[:, q, :])

        def plane_with_stage(name, cols):
            both = tile(name, [P, QUADS * cols], U8)
            nc.vector.memset(both[:, 0:cols].bitcast(I32), 0)
            return both[:, 0:cols], both[:].bitcast(I32).rearrange("p (q c) -> p q c", q=QUADS)

        def spread_in_place(runs):
            for q in range(1, QUADS):
                nc.vector.tensor_copy(out=runs[QUAD * q:QUAD * q + LIVE, 0, :], in_=runs[0:LIVE, q, :])

        xt_plane = zeroed_plane("xt_plane", T)
        w_plane = zeroed_plane("w_plane", R)
        xo_plane = zeroed_plane("xo_plane", T)
        w0_w2_plane = zeroed_plane("w0_w2_plane", 2 * R)
        wb_wc_plane, wb_wc_runs = plane_with_stage("wb_wc_plane", 2 * N)

        warm_in = tile("warm_in", [P, 1], F32)
        nc.gpsimd.memset(warm_in[:], 0.0)
        warm_out = tile("warm_out", [P, 1], F32)
        nc.scalar.activation(out=warm_out[:], in_=warm_in[:], func=ACT.Sigmoid)

        identity = tile("identity", [P, P], F32)
        make_identity(nc, identity[:])

        xo_stage = tile("xo_stage", [LIVE, QUADS, T // WORD], I32)
        nc.sync.dma_start(out=xo_stage[:], in_=scale_rows(xo_scales))
        note_list = load_list("note_list", offs2)
        w0_w2_stage = tile("w0_w2_stage", [LIVE, QUADS, 2 * R // WORD], I32)
        nc.sync.dma_start(out=w0_w2_stage[:, :, 0:R // WORD], in_=scale_rows(w0_scales))
        nc.sync.dma_start(out=w0_w2_stage[:, :, R // WORD:2 * R // WORD], in_=scale_rows(w2_scales))
        xo_sb = load_words("xo_sb", xo_words, T, U32)
        w0_sb = load_words("w0_sb", w0_words, 2 * R, U8)
        load_plane(xt_plane, xt_scales)
        token_list = load_list("token_list", offs)
        w2_sb = load_words("w2_sb", w2_words, R, U32)
        xt_sb = load_words("xt_sb", xt_words, T, U16)
        w_sb = load_words("w_sb", w_words, R, U32)
        load_plane(w_plane, w_scales)
        nc.sync.dma_start(out=wb_wc_runs[0:LIVE, :, 0:N // WORD], in_=scale_rows(wb_scales))
        nc.sync.dma_start(out=wb_wc_runs[0:LIVE, :, N // WORD:2 * N // WORD], in_=scale_rows(wc_scales))
        wb_sb = load_words("wb_sb", wb_words, 2 * N, U8)
        wc_sb = load_words("wc_sb", wc_words, N, U32)
        gate_lists = load_list("gate_lists", offs4)
        weighted_lists = load_list("weighted_lists", offs3)
        q_list = load_list("q_list", offs5)
        per_feature = []
        with nc.allow_non_contiguous_dma(reason="column c holds the value of output feature 128 c + p on partition p"):
            for name, src in (("sp_sb", sp), ("bo_sb", bo), ("so_sb", so)):
                values = tile(name, [P, N_TILES], F32)
                nc.sync.dma_start(out=values[:], in_=src.rearrange("(c p) o -> p (c o)", p=P))
                per_feature.append(values)
        sp_sb, bo_sb, so_sb = per_feature

        spread_rows(xo_plane, xo_stage)
        spread_rows(w0_w2_plane, w0_w2_stage)
        w0_plane = w0_w2_plane[:, 0:R]
        w2_plane = w0_w2_plane[:, R:2 * R]
        note_scales = tile("note_scales", [P, J], U8)
        nc.vector.tensor_copy(out=note_scales[:], in_=xo_plane[:].indirect(note_list[:]))
        note_words = [tile("note_words%d" % h, [P, P], U32) for h in range(HALVES)]
        b_ps = [psum.tile([P, R], F32, name="b_ps%d" % h) for h in range(HALVES)]
        a_ps = [psum.tile([P, R], F32, name="a_ps%d" % h) for h in range(HALVES)]
        b_sb = [tile("b_sb%d" % h, [P, PACK, P], F32) for h in range(HALVES)]
        for h in range(HALVES):
            nc.vector.tensor_copy(out=note_words[h][:], in_=xo_sb[:].indirect(list_half(note_list, h)))
            nc.tensor.matmul_mx(a_ps[h][:], lhsT=note_words[h][:].bitcast(E4M3), lhsT_scale=note_scales[:, block(h)],
                                rhs=w0_sb[:].bitcast(E2M1), rhs_scale=w0_plane, start=True, stop=False)
        for h in range(HALVES):
            nc.tensor.matmul_mx(b_ps[h][:], lhsT=note_words[h][:].bitcast(E4M3), lhsT_scale=note_scales[:, block(h)],
                                rhs=w2_sb[:].bitcast(E5M2), rhs_scale=w2_plane, start=True, stop=True)
            nc.scalar.copy(out=b_sb[h][:], in_=b_ps[h][:].rearrange("j (m t) -> j t m", t=PACK))

        token_scales = tile("token_scales", [P, J], U8)
        nc.vector.tensor_copy(out=token_scales[:], in_=xt_plane[:].indirect(token_list[:]))
        token_words = [tile("token_words%d" % h, [P, P], U16) for h in range(HALVES)]
        for h in range(HALVES):
            nc.vector.tensor_copy(out=token_words[h][:], in_=xt_sb[:].indirect(list_half(token_list, h)))
            nc.tensor.matmul_mx(a_ps[h][:], lhsT=token_words[h][:].bitcast(E2M1), lhsT_scale=token_scales[:, block(h)],
                                rhs=w_sb[:].bitcast(E4M3), rhs_scale=w_plane[:], start=False, stop=True)
        spread_in_place(wb_wc_runs)
        wb_plane = wb_wc_plane[:, 0:N]
        wc_plane = wb_wc_plane[:, N:2 * N]

        turned = [psum.tile([P, PACK, P], F32, name="turned%d" % h) for h in range(HALVES)]
        for h in range(HALVES):
            a_by_t = a_ps[h][:].rearrange("j (m t) -> j t m", t=PACK)
            for pair in range(PACK // 2):
                ts = slice(2 * pair, 2 * pair + 2)
                diff = tile("diff%d%d" % (h, pair), [P, 2, P], F32)
                nc.vector.tensor_tensor(out=diff[:], in0=a_by_t[:, ts], in1=b_sb[h][:, ts], op=ALU.subtract)
                for e in range(2):
                    nc.tensor.transpose(turned[h][:, 2 * pair + e, :], diff[:, e, :], identity[:])

        p_sb = [tile("p_sb%d" % c, [P, J], F32) for c in range(N_TILES)]
        q_sb = tile("q_sb", [P, N_TILES, J], F32)
        first_half_ps = psum.tile([P, 2 * N_TILES, P], F32, name="first_half_ps")
        last_half_ps = psum.tile([P, P], F32, name="last_half_ps")
        p_ps = [[first_half_ps[:, 0, :], first_half_ps[:, 1, :]], [last_half_ps[:], b_ps[0][:, 0:P]]]
        q_ps = [first_half_ps[:, N_TILES:2 * N_TILES, :],
                b_ps[1][:, 0:N_TILES * P].rearrange("n (c j) -> n c j", c=N_TILES)]
        for h in range(HALVES):
            hid = tile("hid%d" % h, [P, P, PACK], BF16)
            nc.scalar.activation(out=hid[:], in_=turned[h][:].rearrange("m t j -> m j t"), func=ACT.Abs)
            hid_words = tile("hid_words%d" % h, [P, P], U32)
            hid_plane = tile("hid_plane%d" % h, [P, P], U8)
            nc.vector.quantize_mx(out=hid_words[:].bitcast(E5M2), scales=hid_plane[:],
                                  in_=hid[:].rearrange("m j t -> m (j t)"))
            for c in range(N_TILES):
                nc.tensor.matmul_mx(p_ps[h][c], lhsT=wb_sb[:, 2 * P * c:2 * P * (c + 1)].bitcast(E2M1),
                                    lhsT_scale=wb_plane[:, block(c)], rhs=hid_words[:].bitcast(E5M2),
                                    rhs_scale=hid_plane[:], start=True, stop=True)
            for c in range(N_TILES):
                nc.tensor.matmul_mx(q_ps[h][:, c, :], lhsT=wc_sb[:, block(c)].bitcast(E5M2),
                                    lhsT_scale=wc_plane[:, block(c)], rhs=hid_words[:].bitcast(E5M2),
                                    rhs_scale=hid_plane[:], start=True, stop=True)

        for c in range(N_TILES):
            nc.scalar.copy(out=p_sb[c][:, block(0)], in_=p_ps[0][c])
        nc.vector.tensor_copy(out=q_sb[:, :, block(0)], in_=q_ps[0])
        nc.scalar.copy(out=p_sb[0][:, block(1)], in_=p_ps[1][0])
        nc.vector.tensor_copy(out=p_sb[1][:, block(1)], in_=p_ps[1][1])
        nc.vector.tensor_copy(out=q_sb[:, :, block(1)], in_=q_ps[1])

        for c in range(N_TILES):
            gate = tile("gate%d" % c, [P, O], F32)
            nc.scalar.activation(out=gate[:], in_=p_sb[c][:].indirect(gate_lists[:]), func=ACT.Sigmoid,
                                 bias=bo_sb[:, c:c + 1], scale=sp_sb[:, c:c + 1])
            weighted = tile("weighted%d" % c, [P, O], F32)
            nc.scalar.activation(out=weighted[:], in_=p_sb[c][:].indirect(weighted_lists[:]), func=ACT.Copy,
                                 scale=so_sb[:, c:c + 1])
            picked = tile("picked%d" % c, [P, O], F32)
            nc.vector.tensor_copy(out=picked[:], in_=q_sb[:, c, :].indirect(q_list[:]))
            gated = tile("gated%d" % c, [P, O], F32)
            nc.vector.tensor_tensor(out=gated[:], in0=weighted[:], in1=gate[:], op=ALU.mult)
            result = tile("result%d" % c, [P, O], F32)
            nc.vector.tensor_tensor(out=result[:], in0=gated[:], in1=picked[:], op=ALU.subtract)
            nc.sync.dma_start(out=out[block(c), :], in_=result[:])
